import numpy as np
import ml_dtypes


def mxq(x, axis, fmt="e4m3"):
    dtype, down = {"e4m3": (ml_dtypes.float8_e4m3fn, 7), "e5m2": (ml_dtypes.float8_e5m2, 14)}[fmt]
    v = np.moveaxis(np.asarray(x, np.float32).astype(ml_dtypes.bfloat16).astype(np.float64), axis, -1)
    blocks = v.reshape(v.shape[:-1] + (-1, 32))
    amax = np.abs(blocks).max(-1, keepdims=True)
    byte = np.maximum(np.where(amax > 0, np.frexp(amax)[1] - 1 + 127, 0) - down, 1)
    scale = np.exp2(byte - 127.0)
    codes = (blocks / scale).astype(np.float32).astype(dtype).astype(np.float64)
    return np.moveaxis((codes * scale).reshape(v.shape), -1, axis)


WIDE = False


def mx_kscale(k):
    if not WIDE:
        return np.ones(k)
    levels = np.array([30, -30])
    if k % 512:
        return np.exp2(np.random.permutation(np.resize(levels, k // 32))).repeat(32)
    a = np.empty((k // 512, 16))
    for p in range(k // 512):
        a[p, :8] = np.random.permutation(np.resize(levels, 8))
        for g in range(8):
            far = levels[np.abs(levels - a[p, g]) >= 10]
            a[p, g + 8] = far[np.random.randint(len(far))]
    return np.exp2(a.ravel()).repeat(32)


def f64(x):
    return np.asarray(x).astype(np.float64)


def striped(idx):
    return np.tile(idx.reshape(-1, 16).T, (8, 1)).astype(np.uint16)


def unstriped(offs):
    return offs[:16].T.reshape(-1).astype(np.int64)


E2M1 = np.array([0.0, 0.5, 1.0, 1.5, 2.0, 3.0, 4.0, 6.0, -0.0, -0.5, -1.0, -1.5, -2.0, -3.0, -4.0, -6.0])


def pack_weight(w, fmt):
    k, n = w.shape
    w = f64(np.asarray(w, np.float32).astype(ml_dtypes.bfloat16)).reshape(k // 32, 32, n)
    amax = np.abs(w).max(1)
    if fmt == "e4m3":
        byte = np.frexp(amax)[1] - 1 + 127 - 7
    elif fmt == "e5m2":
        byte = np.frexp(amax)[1] - 1 + 127 - 14
    else:
        mant, ex = np.frexp(amax / 6.0)
        byte = np.where(mant > 0.5, ex, ex - 1) + 127
    byte = np.clip(np.where(amax > 0, byte, 1), 1, 254)
    scaled = (w * np.exp2(127.0 - byte)[:, None, :]).reshape(k, n).astype(np.float32)
    by_word = np.ascontiguousarray(scaled.reshape(k // 512, 128, 4, n).transpose(0, 1, 3, 2))
    if fmt == "e4m3":
        words = by_word.astype(ml_dtypes.float8_e4m3fn).view(np.uint8)
    elif fmt == "e5m2":
        words = by_word.astype(ml_dtypes.float8_e5m2).view(np.uint8)
    else:
        c = by_word.astype(ml_dtypes.float4_e2m1fn).view(np.uint8) & 0xF
        words = (c[..., 0::2] | (c[..., 1::2] << 4)).reshape(k // 512, 128, 2 * n)
    return np.ascontiguousarray(words), np.ascontiguousarray(byte.astype(np.uint8).reshape(k // 512, 16, n))


def unpack_weight(words, scales, fmt):
    g, _, n = scales.shape
    words = np.ascontiguousarray(words).reshape(g, 128, n, -1)
    if fmt == "e4m3":
        vals = words.view(ml_dtypes.float8_e4m3fn).astype(np.float64)
    elif fmt == "e5m2":
        vals = words.view(ml_dtypes.float8_e5m2).astype(np.float64)
    else:
        nib = np.empty((g, 128, n, 4), np.uint8)
        nib[..., 0::2] = words & 0xF
        nib[..., 1::2] = words >> 4
        vals = E2M1[nib]
    vals = vals * np.repeat(np.exp2(scales.astype(np.float64) - 127.0), 8, axis=1)[..., None]
    return vals.transpose(0, 1, 3, 2).reshape(g * 512, n)


def d_silu(v):
    s = 1.0 / (1.0 + np.exp(-np.maximum(v, -700.0)))
    return s * (1.0 + v * (1.0 - s))


K, T, E, C, H, N = 384, 1024, 4, 512, 512, 512


def by_expert(wq, xq):
    return np.concatenate([wq[e].T @ xq[:, e * C:(e + 1) * C] for e in range(E)], axis=1)


def setup_inputs():
    n = np.random.standard_normal
    s = mx_kscale(N)[:, None]
    u = mx_kscale(H)
    first = np.random.permutation(np.repeat(np.arange(E), T // E))
    second = (first + 1 + np.random.permutation(np.repeat(np.arange(E - 1), -(-T // (E - 1)))[:T])) % E
    while np.bincount(second, minlength=E).max() != T // E:
        load = np.bincount(second, minlength=E); hi, lo = int(load.argmax()), int(load.argmin())
        t = np.flatnonzero((second == hi) & (first != lo))[0]; second[t] = lo
    slot_token = np.empty(E * C, np.int64); pos = np.empty((2, T), np.int64); fill = np.zeros(E, np.int64)
    place = np.stack([np.random.permutation(C) for _ in range(E)])
    for r, deal in enumerate((first, second)):
        for t in np.random.permutation(T):
            e = deal[t]; j = e * C + place[e, fill[e]]; fill[e] += 1; slot_token[j] = t; pos[r, t] = j
    g = np.random.uniform(0.2, 0.8, T)
    w_slot = np.empty(E * C); w_slot[pos[0]] = g; w_slot[pos[1]] = 1.0 - g
    dy = pack_weight(n((N, T)) * s, "e5m2")
    w2 = [pack_weight(m, "e2m1") for m in n((E, N, H)) / np.sqrt(N) / s[None] * u[None, None, :]]
    w1 = [pack_weight(m, "e2m1") for m in n((E, H, K)) / np.sqrt(H) / u[None, :, None]]
    return {
        "dy_words": dy[0],
        "dy_scales": dy[1],
        "a": n((H, E * C)).astype(np.float32),
        "w2_words": np.stack([m[0] for m in w2]),
        "w2_scales": np.stack([m[1] for m in w2]),
        "w1_words": np.stack([m[0] for m in w1]),
        "w1_scales": np.stack([m[1] for m in w1]),
        "gate": np.tile(w_slot, (H, 1)).astype(np.float32),
        "offs": striped(slot_token),
        "pos1": striped(pos[0]),
        "pos2": striped(pos[1]),
    }


def reference(dy_words, dy_scales, a, w2_words, w2_scales, w1_words, w1_scales, gate, offs, pos1, pos2):
    idx = unstriped(offs)
    w2 = np.stack([unpack_weight(w2_words[e], w2_scales[e], "e2m1") for e in range(E)])
    w1 = np.stack([unpack_weight(w1_words[e], w1_scales[e], "e2m1") for e in range(E)])
    gq = unpack_weight(dy_words, dy_scales, "e5m2")[:, idx]
    dh = f64(gate) * by_expert(w2, gq)
    da = dh * d_silu(f64(a))
    dx = by_expert(w1, mxq(da, 0, "e5m2"))
    return dx[:, unstriped(pos1)] + dx[:, unstriped(pos2)]

@@ -1,0 +1,197 @@
+from contextlib import ExitStack
+
+import concourse.mybir as mybir
+from concourse.masks import make_identity
+
+K, T, E, C, H, N = 384, 1024, 4, 512, 512, 512
+S = E * C
+FLOPS = 2 * S * (N * H + H * K)
+BYTES = (N * T + N * T // 32 + 4 * H * S + E * (N * H + H * K) // 2 + E * (N * H + H * K) // 32
+         + 4 * S + 128 * 2 * (S + 2 * T) // 16 + 4 * K * T)
+
+F32 = mybir.dt.float32
+BF16 = mybir.dt.bfloat16
+I32 = mybir.dt.int32
+U32 = mybir.dt.uint32
+U16 = mybir.dt.uint16
+U8 = mybir.dt.uint8
+E5M2X4 = mybir.dt.float8_e5m2_x4
+E2M1X4 = mybir.dt.float4_e2m1fn_x4
+ALU = mybir.AluOpType
+ACT = mybir.ActivationFunctionType
+
+P = 128
+PACK = 4
+LIST_COL = 16
+BLOCKS = S // P
+PER_EXPERT = C // P
+ROW_BLOCKS = K // P
+BANKS = 4
+HALF = T // 2
+
+
+def tile_moe_bdx_mlp_silu_kernel(
+    tc, dy_words, dy_scales, a, w2_words, w2_scales, w1_words, w1_scales, gate, offs, pos1, pos2, out
+):
+    nc = tc.nc
+    with ExitStack() as ctx:
+        keep = ctx.enter_context(tc.tile_pool(name="keep", bufs=1))
+        psum = ctx.enter_context(tc.psum_pool(name="psum", bufs=1))
+
+        def sbuf(name, shape, dtype):
+            return keep.tile(shape, dtype, name=name, align_bytes=64)
+
+        def load_scale_rows(plane, rows):
+            by_row = rows.rearrange("g (q r) n -> r q g n", r=4)
+            for r in range(4):
+                nc.sync.dma_start(out=plane[r:P:32, :, :].bitcast(I32), in_=by_row[r].bitcast(I32))
+
+        offs_sb = keep.tile([P, S // LIST_COL], U16, name="offs_sb")
+        pos1_sb = keep.tile([P, T // LIST_COL], U16, name="pos1_sb")
+        pos2_sb = keep.tile([P, T // LIST_COL], U16, name="pos2_sb")
+        dy_w = sbuf("dy_w", [P, T], I32)
+        dy_s = sbuf("dy_s", [P, 1, T], U8)
+        w2_w = sbuf("w2_w", [P, E, 2 * H], U8)
+        w2_s = sbuf("w2_s", [P, E, H], U8)
+        w1_w = sbuf("w1_w", [P, E, 2 * K], U8)
+        w1_s = sbuf("w1_s", [P, E, K], U8)
+        gate_rows = sbuf("gate_rows", [P, P], F32)
+        neg_gate = sbuf("neg_gate", [P, BLOCKS], F32)
+        act_const = sbuf("act_const", [P, 1], F32)
+        ident = sbuf("ident", [P, P], F32)
+        a_sb = [sbuf("a_sb%d" % e, [P, PACK, C], F32) for e in range(E)]
+        g_w = [sbuf("g_w%d" % e, [P, C], U32) for e in range(E)]
+        g_s = [sbuf("g_s%d" % e, [P, C], U8) for e in range(E)]
+        act_ring = [sbuf("act%d" % i, [P, H], F32) for i in range(BLOCKS)]
+        part = [sbuf("part%d" % j, [P, H], F32) for j in range(BLOCKS)]
+        da = [sbuf("da%d" % i, [P, H], BF16) for i in range(3)]
+        da_w = [sbuf("da_w%d" % e, [P, C], U32) for e in range(E)]
+        da_s = [sbuf("da_s%d" % e, [P, C], U8) for e in range(E)]
+        dx = [sbuf("dx%d" % kb, [P, S], F32) for kb in range(ROW_BLOCKS)]
+        first = [sbuf("first%d" % i, [P, HALF], F32) for i in range(2)]
+        total = [sbuf("total%d" % i, [P, HALF], F32) for i in range(2 * ROW_BLOCKS)]
+        turn_banks = [psum.tile([P, H], F32, name="turn%d" % i) for i in range(BANKS)]
+        mx_banks = [psum.tile([P, C], F32, name="mx%d" % i) for i in range(BANKS)]
+
+        nc.gpsimd.memset(dy_s[:].bitcast(I32), 0)
+        nc.gpsimd.memset(act_const[:], 0.0)
+        nc.vector.memset(gate_rows[:], 0.0)
+        nc.vector.memset(w2_s[:].bitcast(I32), 0)
+        nc.vector.memset(w1_s[:].bitcast(I32), 0)
+        make_identity(nc, ident[:])
+
+        a_rows = a.rearrange("(p t) s -> p t s", t=PACK)
+
+        def load_a(e):
+            nc.sync.dma_start(out=a_sb[e][:], in_=a_rows[:, :, e * C:(e + 1) * C])
+
+        nc.sync.dma_start(out=dy_w[:], in_=dy_words[0].rearrange("p t d -> p (t d)").bitcast(I32))
+        nc.sync.dma_start(offs_sb[:], offs)
+        load_scale_rows(dy_s, dy_scales)
+        load_a(0)
+        load_a(1)
+        nc.sync.dma_start(out=w2_w[:].bitcast(I32), in_=w2_words.rearrange("e o p b -> p (e o) b").bitcast(I32))
+        load_a(2)
+        nc.sync.dma_start(out=gate_rows[0:BLOCKS, :], in_=gate[0].rearrange("(j p) -> j p", p=P))
+        load_scale_rows(w2_s, w2_scales.rearrange("e o f n -> (e o) f n"))
+        load_a(3)
+        load_scale_rows(w1_s, w1_scales.rearrange("e o f n -> (e o) f n"))
+        nc.sync.dma_start(out=w1_w[:].bitcast(I32), in_=w1_words.rearrange("e o p b -> p (e o) b").bitcast(I32))
+        nc.sync.dma_start(pos1_sb[:], pos1)
+        nc.sync.dma_start(pos2_sb[:], pos2)
+
+        gate_bank = mx_banks[BANKS - 1]
+        nc.tensor.transpose(gate_bank[:, 0:P], gate_rows[:], ident[:])
+        nc.scalar.activation(neg_gate[:], gate_bank[:, 0:BLOCKS], ACT.Copy, scale=-1.0)
+
+        cols = C // LIST_COL
+        for e in range(E):
+            slots = offs_sb[:, e * cols:(e + 1) * cols]
+            nc.vector.tensor_copy(g_w[e][:], dy_w[:].bitcast(U32).indirect(slots))
+            nc.vector.tensor_copy(g_s[e][:], dy_s[:, 0, :].indirect(slots))
+
+        for j in range(BLOCKS):
+            e, b = divmod(j, PER_EXPERT)
+            block = slice(b * P, (b + 1) * P)
+            a_turned = turn_banks[j % BANKS]
+            for t in range(PACK):
+                nc.tensor.transpose(a_turned[:, t * P:(t + 1) * P], a_sb[e][:, t, block], ident[:])
+            nc.scalar.activation(act_ring[j][:], a_turned[:], ACT.Sigmoid, bias=act_const[:])
+
+        for j in range(BLOCKS):
+            e, b = divmod(j, PER_EXPERT)
+            block = slice(b * P, (b + 1) * P)
+            sig = act_ring[j]
+            dh = mx_banks[j % BANKS]
+            nc.tensor.matmul_mx(
+                out=dh[:],
+                lhsT=g_w[e][:, block].bitcast(E5M2X4), lhsT_scale=g_s[e][:, block],
+                rhs=w2_w[:, e, :].bitcast(E2M1X4), rhs_scale=w2_s[:, e, :],
+                start=True, stop=True,
+            )
+            nc.vector.scalar_tensor_tensor(
+                out=part[j][:].rearrange("s (t p) -> s t p", t=PACK),
+                in0=dh[:].rearrange("s (p t) -> s t p", t=PACK),
+                scalar=neg_gate[:, j:j + 1],
+                in1=sig[:].rearrange("s (t p) -> s t p", t=PACK),
+                op0=ALU.mult, op1=ALU.mult,
+            )
+
+        nc.gpsimd.memset(act_const[:], -1.0)
+
+        def finish_da(j):
+            e, b = divmod(j, PER_EXPERT)
+            part_turned = turn_banks[j % BANKS]
+            for t in range(PACK):
+                nc.tensor.transpose(part_turned[:, t * P:(t + 1) * P], part[j][:, t * P:(t + 1) * P], ident[:])
+            silu_neg = act_ring[j]
+            nc.scalar.activation(
+                silu_neg[:].rearrange("p (c u t) -> p c t u", u=2, t=PACK),
+                a_sb[e][:, :, b * P:(b + 1) * P].rearrange("p t (c u) -> p c t u", u=2),
+                ACT.Silu, scale=act_const[:],
+            )
+            nc.vector.scalar_tensor_tensor(
+                out=da[j % 3][:].rearrange("p (s t) -> p s t", t=PACK),
+                in0=silu_neg[:].rearrange("p (s t) -> p s t", t=PACK),
+                scalar=1.0,
+                in1=part_turned[:].rearrange("p (t s) -> p s t", t=PACK),
+                op0=ALU.subtract, op1=ALU.mult,
+            )
+
+        def quantize_da(j):
+            e, b = divmod(j, PER_EXPERT)
+            block = slice(b * P, (b + 1) * P)
+            nc.vector.quantize_mx(out=da_w[e][:, block].bitcast(E5M2X4), scales=da_s[e][:, block], in_=da[j % 3][:])
+
+        def second_product(kb, e):
+            acc = mx_banks[(kb * E + e) % BANKS]
+            nc.tensor.matmul_mx(
+                out=acc[:],
+                lhsT=w1_w[:, e, 2 * kb * P:2 * (kb + 1) * P].bitcast(E2M1X4),
+                lhsT_scale=w1_s[:, e, kb * P:(kb + 1) * P],
+                rhs=da_w[e][:].bitcast(E5M2X4), rhs_scale=da_s[e][:],
+                start=True, stop=True,
+            )
+            nc.scalar.copy(dx[kb][:, e * C:(e + 1) * C], acc[:])
+
+        for step in range(BLOCKS + 1):
+            if step < BLOCKS:
+                finish_da(step)
+            if step > 0:
+                quantize_da(step - 1)
+                if step % PER_EXPERT == 0:
+                    second_product(0, step // PER_EXPERT - 1)
+        for kb in range(1, ROW_BLOCKS):
+            for e in range(E):
+                second_product(kb, e)
+
+        cols = HALF // LIST_COL
+        for kb in range(ROW_BLOCKS):
+            for h in range(2):
+                nc.vector.tensor_copy(first[h][:], dx[kb][:].indirect(pos1_sb[:, h * cols:(h + 1) * cols]))
+            for h in range(2):
+                both = total[2 * kb + h]
+                nc.vector.tensor_tensor(
+                    both[:], dx[kb][:].indirect(pos2_sb[:, h * cols:(h + 1) * cols]), first[h][:], ALU.add
+                )
+                nc.sync.dma_start(out=out[kb * P:(kb + 1) * P, h * HALF:(h + 1) * HALF], in_=both[:])

@@ -28,6 +28,7 @@ PER_EXPERT = C // P
 ROW_BLOCKS = K // P
 BANKS = 4
 HALF = T // 2
+PIECES = 2 * ROW_BLOCKS
 
 
 def tile_moe_bdx_mlp_silu_kernel(
@@ -51,7 +52,7 @@ def tile_moe_bdx_mlp_silu_kernel(
         pos2_sb = keep.tile([P, T // LIST_COL], U16, name="pos2_sb")
         dy_w = sbuf("dy_w", [P, T], I32)
         dy_s = sbuf("dy_s", [P, 1, T], U8)
-        w2_w = sbuf("w2_w", [P, E, 2 * H], U8)
+        w2_w = [sbuf("w2_w%d" % e, [P, 2 * H], U8) for e in range(E)]
         w2_s = sbuf("w2_s", [P, E, H], U8)
         w1_w = sbuf("w1_w", [P, E, 2 * K], U8)
         w1_s = sbuf("w1_s", [P, E, K], U8)
@@ -69,7 +70,7 @@ def tile_moe_bdx_mlp_silu_kernel(
         da_s = [sbuf("da_s%d" % e, [P, C], U8) for e in range(E)]
         dx = [sbuf("dx%d" % kb, [P, S], F32) for kb in range(ROW_BLOCKS)]
         first = [sbuf("first%d" % i, [P, HALF], F32) for i in range(2)]
-        total = [sbuf("total%d" % i, [P, HALF], F32) for i in range(2 * ROW_BLOCKS)]
+        total = [sbuf("total%d" % i, [P, HALF], F32) for i in range(PIECES)]
         turn_banks = [psum.tile([P, H], F32, name="turn%d" % i) for i in range(BANKS)]
         mx_banks = [psum.tile([P, C], F32, name="mx%d" % i) for i in range(BANKS)]
 
@@ -85,16 +86,21 @@ def tile_moe_bdx_mlp_silu_kernel(
         def load_a(e):
             nc.sync.dma_start(out=a_sb[e][:], in_=a_rows[:, :, e * C:(e + 1) * C])
 
+        def load_w2(e):
+            nc.sync.dma_start(out=w2_w[e][:].bitcast(I32), in_=w2_words[e, 0].bitcast(I32))
+
         nc.sync.dma_start(out=dy_w[:], in_=dy_words[0].rearrange("p t d -> p (t d)").bitcast(I32))
         nc.sync.dma_start(offs_sb[:], offs)
         load_scale_rows(dy_s, dy_scales)
         load_a(0)
         load_a(1)
-        nc.sync.dma_start(out=w2_w[:].bitcast(I32), in_=w2_words.rearrange("e o p b -> p (e o) b").bitcast(I32))
         load_a(2)
         nc.sync.dma_start(out=gate_rows[0:BLOCKS, :], in_=gate[0].rearrange("(j p) -> j p", p=P))
         load_scale_rows(w2_s, w2_scales.rearrange("e o f n -> (e o) f n"))
+        load_w2(0)
         load_a(3)
+        for e in range(1, E):
+            load_w2(e)
         load_scale_rows(w1_s, w1_scales.rearrange("e o f n -> (e o) f n"))
         nc.sync.dma_start(out=w1_w[:].bitcast(I32), in_=w1_words.rearrange("e o p b -> p (e o) b").bitcast(I32))
         nc.sync.dma_start(pos1_sb[:], pos1)
@@ -106,9 +112,9 @@ def tile_moe_bdx_mlp_silu_kernel(
 
         cols = C // LIST_COL
         for e in range(E):
-            slots = offs_sb[:, e * cols:(e + 1) * cols]
-            nc.vector.tensor_copy(g_w[e][:], dy_w[:].bitcast(U32).indirect(slots))
-            nc.vector.tensor_copy(g_s[e][:], dy_s[:, 0, :].indirect(slots))
+            nc.vector.tensor_copy(g_w[e][:], dy_w[:].bitcast(U32).indirect(offs_sb[:, e * cols:(e + 1) * cols]))
+        for e in range(E):
+            nc.vector.tensor_copy(g_s[e][:], dy_s[:, 0, :].indirect(offs_sb[:, e * cols:(e + 1) * cols]))
 
         for j in range(BLOCKS):
             e, b = divmod(j, PER_EXPERT)
@@ -126,7 +132,7 @@ def tile_moe_bdx_mlp_silu_kernel(
             nc.tensor.matmul_mx(
                 out=dh[:],
                 lhsT=g_w[e][:, block].bitcast(E5M2X4), lhsT_scale=g_s[e][:, block],
-                rhs=w2_w[:, e, :].bitcast(E2M1X4), rhs_scale=w2_s[:, e, :],
+                rhs=w2_w[e][:].bitcast(E2M1X4), rhs_scale=w2_s[:, e, :],
                 start=True, stop=True,
             )
             nc.vector.scalar_tensor_tensor(
@@ -164,7 +170,7 @@ def tile_moe_bdx_mlp_silu_kernel(
             nc.vector.quantize_mx(out=da_w[e][:, block].bitcast(E5M2X4), scales=da_s[e][:, block], in_=da[j % 3][:])
 
         def second_product(kb, e):
-            acc = mx_banks[(kb * E + e) % BANKS]
+            acc = mx_banks[e] if kb == 0 else turn_banks[e]
             nc.tensor.matmul_mx(
                 out=acc[:],
                 lhsT=w1_w[:, e, 2 * kb * P:2 * (kb + 1) * P].bitcast(E2M1X4),

@@ -28,6 +28,10 @@ PER_EXPERT = C // P
 ROW_BLOCKS = K // P
 BANKS = 4
 HALF = T // 2
+A_WIDTH = 256
+A_LOADS = S // A_WIDTH
+LAST = E - 1
+ON_VECTOR = BLOCKS - 3
 PIECES = 2 * ROW_BLOCKS
 
 
@@ -60,7 +64,9 @@ def tile_moe_bdx_mlp_silu_kernel(
         neg_gate = sbuf("neg_gate", [P, BLOCKS], F32)
         act_const = sbuf("act_const", [P, 1], F32)
         ident = sbuf("ident", [P, P], F32)
-        a_sb = [sbuf("a_sb%d" % e, [P, PACK, C], F32) for e in range(E)]
+        a_sb = [sbuf("a_sb%d" % i, [P, PACK, A_WIDTH], F32) for i in range(A_LOADS)]
+        a_block = [a_sb[i][:, :, c:c + P] for i in range(A_LOADS) for c in range(0, A_WIDTH, P)]
+        dh_gated = {j: sbuf("dh_gated%d" % j, [P, H], F32) for j in range(ON_VECTOR, BLOCKS)}
         g_w = [sbuf("g_w%d" % e, [P, C], U32) for e in range(E)]
         g_s = [sbuf("g_s%d" % e, [P, C], U8) for e in range(E)]
         act_ring = [sbuf("act%d" % i, [P, H], F32) for i in range(BLOCKS)]
@@ -83,23 +89,25 @@ def tile_moe_bdx_mlp_silu_kernel(
 
         a_rows = a.rearrange("(p t) s -> p t s", t=PACK)
 
-        def load_a(e):
-            nc.sync.dma_start(out=a_sb[e][:], in_=a_rows[:, :, e * C:(e + 1) * C])
+        def load_a(i):
+            nc.sync.dma_start(out=a_sb[i][:], in_=a_rows[:, :, i * A_WIDTH:(i + 1) * A_WIDTH])
 
         def load_w2(e):
             nc.sync.dma_start(out=w2_w[e][:].bitcast(I32), in_=w2_words[e, 0].bitcast(I32))
 
-        nc.sync.dma_start(out=dy_w[:], in_=dy_words[0].rearrange("p t d -> p (t d)").bitcast(I32))
         nc.sync.dma_start(offs_sb[:], offs)
         load_scale_rows(dy_s, dy_scales)
         load_a(0)
         load_a(1)
+        nc.sync.dma_start(out=dy_w[:], in_=dy_words[0].rearrange("p t d -> p (t d)").bitcast(I32))
         load_a(2)
-        nc.sync.dma_start(out=gate_rows[0:BLOCKS, :], in_=gate[0].rearrange("(j p) -> j p", p=P))
-        load_scale_rows(w2_s, w2_scales.rearrange("e o f n -> (e o) f n"))
-        load_w2(0)
         load_a(3)
-        for e in range(1, E):
+        load_w2(LAST)
+        load_scale_rows(w2_s, w2_scales.rearrange("e o f n -> (e o) f n"))
+        nc.sync.dma_start(out=gate_rows[0:BLOCKS, :], in_=gate[0].rearrange("(j p) -> j p", p=P))
+        load_a(4)
+        for e in range(LAST):
+            load_a(5 + e)
             load_w2(e)
         load_scale_rows(w1_s, w1_scales.rearrange("e o f n -> (e o) f n"))
         nc.sync.dma_start(out=w1_w[:].bitcast(I32), in_=w1_words.rearrange("e o p b -> p (e o) b").bitcast(I32))
@@ -111,23 +119,20 @@ def tile_moe_bdx_mlp_silu_kernel(
         nc.scalar.activation(neg_gate[:], gate_bank[:, 0:BLOCKS], ACT.Copy, scale=-1.0)
 
         cols = C // LIST_COL
-        for e in range(E):
+
+        def gather_words(e):
             nc.vector.tensor_copy(g_w[e][:], dy_w[:].bitcast(U32).indirect(offs_sb[:, e * cols:(e + 1) * cols]))
-        for e in range(E):
+
+        def gather_scales(e):
             nc.vector.tensor_copy(g_s[e][:], dy_s[:, 0, :].indirect(offs_sb[:, e * cols:(e + 1) * cols]))
 
-        for j in range(BLOCKS):
-            e, b = divmod(j, PER_EXPERT)
-            block = slice(b * P, (b + 1) * P)
-            a_turned = turn_banks[j % BANKS]
-            for t in range(PACK):
-                nc.tensor.transpose(a_turned[:, t * P:(t + 1) * P], a_sb[e][:, t, block], ident[:])
-            nc.scalar.activation(act_ring[j][:], a_turned[:], ACT.Sigmoid, bias=act_const[:])
+        for gather in (gather_scales, gather_words):
+            for e in (LAST,) + tuple(range(LAST)):
+                gather(e)
 
-        for j in range(BLOCKS):
+        def first_product(j):
             e, b = divmod(j, PER_EXPERT)
             block = slice(b * P, (b + 1) * P)
-            sig = act_ring[j]
             dh = mx_banks[j % BANKS]
             nc.tensor.matmul_mx(
                 out=dh[:],
@@ -135,25 +140,40 @@ def tile_moe_bdx_mlp_silu_kernel(
                 rhs=w2_w[e][:].bitcast(E2M1X4), rhs_scale=w2_s[:, e, :],
                 start=True, stop=True,
             )
-            nc.vector.scalar_tensor_tensor(
-                out=part[j][:].rearrange("s (t p) -> s t p", t=PACK),
-                in0=dh[:].rearrange("s (p t) -> s t p", t=PACK),
-                scalar=neg_gate[:, j:j + 1],
-                in1=sig[:].rearrange("s (t p) -> s t p", t=PACK),
-                op0=ALU.mult, op1=ALU.mult,
+            return dh[:].rearrange("s (p t) -> s t p", t=PACK)
+
+        for j in range(ON_VECTOR, BLOCKS):
+            nc.scalar.activation(
+                dh_gated[j][:].rearrange("s (t p) -> s t p", t=PACK), first_product(j),
+                ACT.Copy, scale=neg_gate[:, j:j + 1],
             )
 
-        nc.gpsimd.memset(act_const[:], -1.0)
+        for j in range(BLOCKS):
+            a_turned = turn_banks[j % BANKS]
+            for t in range(PACK):
+                nc.tensor.transpose(a_turned[:, t * P:(t + 1) * P], a_block[j][:, t, :], ident[:])
+            nc.scalar.activation(act_ring[j][:], a_turned[:], ACT.Sigmoid, bias=act_const[:])
+        nc.scalar.activation(act_const[:], act_const[:], ACT.Copy, bias=-1.0)
+
+        for j in range(ON_VECTOR):
+            nc.vector.scalar_tensor_tensor(
+                out=part[j][:].rearrange("s (t p) -> s t p", t=PACK),
+                in0=first_product(j),
+                scalar=neg_gate[:, j:j + 1],
+                in1=act_ring[j][:].rearrange("s (t p) -> s t p", t=PACK),
+                op0=ALU.mult, op1=ALU.mult,
+            )
+        for j in range(ON_VECTOR, BLOCKS):
+            nc.gpsimd.tensor_tensor(part[j][:], dh_gated[j][:], act_ring[j][:], ALU.mult)
 
         def finish_da(j):
-            e, b = divmod(j, PER_EXPERT)
             part_turned = turn_banks[j % BANKS]
             for t in range(PACK):
                 nc.tensor.transpose(part_turned[:, t * P:(t + 1) * P], part[j][:, t * P:(t + 1) * P], ident[:])
             silu_neg = act_ring[j]
             nc.scalar.activation(
                 silu_neg[:].rearrange("p (c u t) -> p c t u", u=2, t=PACK),
-                a_sb[e][:, :, b * P:(b + 1) * P].rearrange("p t (c u) -> p c t u", u=2),
+                a_block[j].rearrange("p t (c u) -> p c t u", u=2),
                 ACT.Silu, scale=act_const[:],
             )
             nc.vector.scalar_tensor_tensor(

@@ -71,7 +71,7 @@ def tile_moe_bdx_mlp_silu_kernel(
         g_s = [sbuf("g_s%d" % e, [P, C], U8) for e in range(E)]
         act_ring = [sbuf("act%d" % i, [P, H], F32) for i in range(BLOCKS)]
         part = [sbuf("part%d" % j, [P, H], F32) for j in range(BLOCKS)]
-        da = [sbuf("da%d" % i, [P, H], BF16) for i in range(3)]
+        da = [sbuf("da%d" % e, [P, PACK * C], BF16) for e in range(E)]
         da_w = [sbuf("da_w%d" % e, [P, C], U32) for e in range(E)]
         da_s = [sbuf("da_s%d" % e, [P, C], U8) for e in range(E)]
         dx = [sbuf("dx%d" % kb, [P, S], F32) for kb in range(ROW_BLOCKS)]
@@ -99,8 +99,8 @@ def tile_moe_bdx_mlp_silu_kernel(
         load_scale_rows(dy_s, dy_scales)
         load_a(0)
         load_a(1)
-        nc.sync.dma_start(out=dy_w[:], in_=dy_words[0].rearrange("p t d -> p (t d)").bitcast(I32))
         load_a(2)
+        nc.sync.dma_start(out=dy_w[:], in_=dy_words[0].rearrange("p t d -> p (t d)").bitcast(I32))
         load_a(3)
         load_w2(LAST)
         load_scale_rows(w2_s, w2_scales.rearrange("e o f n -> (e o) f n"))
@@ -167,6 +167,7 @@ def tile_moe_bdx_mlp_silu_kernel(
             nc.gpsimd.tensor_tensor(part[j][:], dh_gated[j][:], act_ring[j][:], ALU.mult)
 
         def finish_da(j):
+            e, b = divmod(j, PER_EXPERT)
             part_turned = turn_banks[j % BANKS]
             for t in range(PACK):
                 nc.tensor.transpose(part_turned[:, t * P:(t + 1) * P], part[j][:, t * P:(t + 1) * P], ident[:])
@@ -177,17 +178,18 @@ def tile_moe_bdx_mlp_silu_kernel(
                 ACT.Silu, scale=act_const[:],
             )
             nc.vector.scalar_tensor_tensor(
-                out=da[j % 3][:].rearrange("p (s t) -> p s t", t=PACK),
+                out=da[e][:, b * H:(b + 1) * H].rearrange("p (s t) -> p s t", t=PACK),
                 in0=silu_neg[:].rearrange("p (s t) -> p s t", t=PACK),
                 scalar=1.0,
                 in1=part_turned[:].rearrange("p (t s) -> p s t", t=PACK),
                 op0=ALU.subtract, op1=ALU.mult,
             )
 
-        def quantize_da(j):
-            e, b = divmod(j, PER_EXPERT)
-            block = slice(b * P, (b + 1) * P)
-            nc.vector.quantize_mx(out=da_w[e][:, block].bitcast(E5M2X4), scales=da_s[e][:, block], in_=da[j % 3][:])
+        def quantize_da(e, start, stop):
+            nc.vector.quantize_mx(
+                out=da_w[e][:, start:stop].bitcast(E5M2X4), scales=da_s[e][:, start:stop],
+                in_=da[e][:, PACK * start:PACK * stop],
+            )
 
         def second_product(kb, e):
             acc = mx_banks[e] if kb == 0 else turn_banks[e]
@@ -200,13 +202,16 @@ def tile_moe_bdx_mlp_silu_kernel(
             )
             nc.scalar.copy(dx[kb][:, e * C:(e + 1) * C], acc[:])
 
-        for step in range(BLOCKS + 1):
-            if step < BLOCKS:
-                finish_da(step)
-            if step > 0:
-                quantize_da(step - 1)
-                if step % PER_EXPERT == 0:
-                    second_product(0, step // PER_EXPERT - 1)
+        for j in range(BLOCKS):
+            e, b = divmod(j, PER_EXPERT)
+            finish_da(j)
+            if b == 0 and e > 0:
+                quantize_da(e - 1, 0, C)
+                second_product(0, e - 1)
+            if b > 0 and e == LAST:
+                quantize_da(LAST, (b - 1) * P, b * P)
+        quantize_da(LAST, C - P, C)
+        second_product(0, LAST)
         for kb in range(1, ROW_BLOCKS):
             for e in range(E):
                 second_product(kb, e)

from contextlib import ExitStack

import concourse.mybir as mybir
from concourse.masks import make_identity

K, T, E, C, H, N = 384, 1024, 4, 512, 512, 512
S = E * C
FLOPS = 2 * S * (N * H + H * K)
BYTES = (N * T + N * T // 32 + 4 * H * S + E * (N * H + H * K) // 2 + E * (N * H + H * K) // 32
         + 4 * S + 128 * 2 * (S + 2 * T) // 16 + 4 * K * T)

F32 = mybir.dt.float32
BF16 = mybir.dt.bfloat16
I32 = mybir.dt.int32
U32 = mybir.dt.uint32
U16 = mybir.dt.uint16
U8 = mybir.dt.uint8
E5M2X4 = mybir.dt.float8_e5m2_x4
E2M1X4 = mybir.dt.float4_e2m1fn_x4
ALU = mybir.AluOpType
ACT = mybir.ActivationFunctionType

P = 128
PACK = 4
LIST_COL = 16
BLOCKS = S // P
PER_EXPERT = C // P
ROW_BLOCKS = K // P
BANKS = 4
HALF = T // 2
A_WIDTH = 256
A_LOADS = S // A_WIDTH
LAST = E - 1
ON_VECTOR = BLOCKS - 3
PIECES = 2 * ROW_BLOCKS


def tile_moe_bdx_mlp_silu_kernel(
    tc, dy_words, dy_scales, a, w2_words, w2_scales, w1_words, w1_scales, gate, offs, pos1, pos2, out
):
    nc = tc.nc
    with ExitStack() as ctx:
        keep = ctx.enter_context(tc.tile_pool(name="keep", bufs=1))
        psum = ctx.enter_context(tc.psum_pool(name="psum", bufs=1))

        def sbuf(name, shape, dtype):
            return keep.tile(shape, dtype, name=name, align_bytes=64)

        def load_scale_rows(plane, rows):
            by_row = rows.rearrange("g (q r) n -> r q g n", r=4)
            for r in range(4):
                nc.sync.dma_start(out=plane[r:P:32, :, :].bitcast(I32), in_=by_row[r].bitcast(I32))

        offs_sb = keep.tile([P, S // LIST_COL], U16, name="offs_sb")
        pos1_sb = keep.tile([P, T // LIST_COL], U16, name="pos1_sb")
        pos2_sb = keep.tile([P, T // LIST_COL], U16, name="pos2_sb")
        dy_w = sbuf("dy_w", [P, T], I32)
        dy_s = sbuf("dy_s", [P, 1, T], U8)
        w2_w = [sbuf("w2_w%d" % e, [P, 2 * H], U8) for e in range(E)]
        w2_s = sbuf("w2_s", [P, E, H], U8)
        w1_w = sbuf("w1_w", [P, E, 2 * K], U8)
        w1_s = sbuf("w1_s", [P, E, K], U8)
        gate_rows = sbuf("gate_rows", [P, P], F32)
        neg_gate = sbuf("neg_gate", [P, BLOCKS], F32)
        act_const = sbuf("act_const", [P, 1], F32)
        ident = sbuf("ident", [P, P], F32)
        a_sb = [sbuf("a_sb%d" % i, [P, PACK, A_WIDTH], F32) for i in range(A_LOADS)]
        a_block = [a_sb[i][:, :, c:c + P] for i in range(A_LOADS) for c in range(0, A_WIDTH, P)]
        dh_gated = {j: sbuf("dh_gated%d" % j, [P, H], F32) for j in range(ON_VECTOR, BLOCKS)}
        g_w = [sbuf("g_w%d" % e, [P, C], U32) for e in range(E)]
        g_s = [sbuf("g_s%d" % e, [P, C], U8) for e in range(E)]
        act_ring = [sbuf("act%d" % i, [P, H], F32) for i in range(BLOCKS)]
        part = [sbuf("part%d" % j, [P, H], F32) for j in range(BLOCKS)]
        da = [sbuf("da%d" % e, [P, PACK * C], BF16) for e in range(E)]
        da_w = [sbuf("da_w%d" % e, [P, C], U32) for e in range(E)]
        da_s = [sbuf("da_s%d" % e, [P, C], U8) for e in range(E)]
        dx = [sbuf("dx%d" % kb, [P, S], F32) for kb in range(ROW_BLOCKS)]
        first = [sbuf("first%d" % i, [P, HALF], F32) for i in range(2)]
        total = [sbuf("total%d" % i, [P, HALF], F32) for i in range(PIECES)]
        turn_banks = [psum.tile([P, H], F32, name="turn%d" % i) for i in range(BANKS)]
        mx_banks = [psum.tile([P, C], F32, name="mx%d" % i) for i in range(BANKS)]

        nc.gpsimd.memset(dy_s[:].bitcast(I32), 0)
        nc.gpsimd.memset(act_const[:], 0.0)
        nc.vector.memset(gate_rows[:], 0.0)
        nc.vector.memset(w2_s[:].bitcast(I32), 0)
        nc.vector.memset(w1_s[:].bitcast(I32), 0)
        make_identity(nc, ident[:])

        a_rows = a.rearrange("(p t) s -> p t s", t=PACK)

        def load_a(i):
            nc.sync.dma_start(out=a_sb[i][:], in_=a_rows[:, :, i * A_WIDTH:(i + 1) * A_WIDTH])

        def load_w2(e):
            nc.sync.dma_start(out=w2_w[e][:].bitcast(I32), in_=w2_words[e, 0].bitcast(I32))

        nc.sync.dma_start(offs_sb[:], offs)
        load_scale_rows(dy_s, dy_scales)
        load_a(0)
        load_a(1)
        load_a(2)
        nc.sync.dma_start(out=dy_w[:], in_=dy_words[0].rearrange("p t d -> p (t d)").bitcast(I32))
        load_a(3)
        load_w2(LAST)
        load_scale_rows(w2_s, w2_scales.rearrange("e o f n -> (e o) f n"))
        nc.sync.dma_start(out=gate_rows[0:BLOCKS, :], in_=gate[0].rearrange("(j p) -> j p", p=P))
        load_a(4)
        for e in range(LAST):
            load_a(5 + e)
            load_w2(e)
        load_scale_rows(w1_s, w1_scales.rearrange("e o f n -> (e o) f n"))
        nc.sync.dma_start(out=w1_w[:].bitcast(I32), in_=w1_words.rearrange("e o p b -> p (e o) b").bitcast(I32))
        nc.sync.dma_start(pos1_sb[:], pos1)
        nc.sync.dma_start(pos2_sb[:], pos2)

        gate_bank = mx_banks[BANKS - 1]
        nc.tensor.transpose(gate_bank[:, 0:P], gate_rows[:], ident[:])
        nc.scalar.activation(neg_gate[:], gate_bank[:, 0:BLOCKS], ACT.Copy, scale=-1.0)

        cols = C // LIST_COL

        def gather_words(e):
            nc.vector.tensor_copy(g_w[e][:], dy_w[:].bitcast(U32).indirect(offs_sb[:, e * cols:(e + 1) * cols]))

        def gather_scales(e):
            nc.vector.tensor_copy(g_s[e][:], dy_s[:, 0, :].indirect(offs_sb[:, e * cols:(e + 1) * cols]))

        for gather in (gather_scales, gather_words):
            for e in (LAST,) + tuple(range(LAST)):
                gather(e)

        def first_product(j):
            e, b = divmod(j, PER_EXPERT)
            block = slice(b * P, (b + 1) * P)
            dh = mx_banks[j % BANKS]
            nc.tensor.matmul_mx(
                out=dh[:],
                lhsT=g_w[e][:, block].bitcast(E5M2X4), lhsT_scale=g_s[e][:, block],
                rhs=w2_w[e][:].bitcast(E2M1X4), rhs_scale=w2_s[:, e, :],
                start=True, stop=True,
            )
            return dh[:].rearrange("s (p t) -> s t p", t=PACK)

        for j in range(ON_VECTOR, BLOCKS):
            nc.scalar.activation(
                dh_gated[j][:].rearrange("s (t p) -> s t p", t=PACK), first_product(j),
                ACT.Copy, scale=neg_gate[:, j:j + 1],
            )

        for j in range(BLOCKS):
            a_turned = turn_banks[j % BANKS]
            for t in range(PACK):
                nc.tensor.transpose(a_turned[:, t * P:(t + 1) * P], a_block[j][:, t, :], ident[:])
            nc.scalar.activation(act_ring[j][:], a_turned[:], ACT.Sigmoid, bias=act_const[:])
        nc.scalar.activation(act_const[:], act_const[:], ACT.Copy, bias=-1.0)

        for j in range(ON_VECTOR):
            nc.vector.scalar_tensor_tensor(
                out=part[j][:].rearrange("s (t p) -> s t p", t=PACK),
                in0=first_product(j),
                scalar=neg_gate[:, j:j + 1],
                in1=act_ring[j][:].rearrange("s (t p) -> s t p", t=PACK),
                op0=ALU.mult, op1=ALU.mult,
            )
        for j in range(ON_VECTOR, BLOCKS):
            nc.gpsimd.tensor_tensor(part[j][:], dh_gated[j][:], act_ring[j][:], ALU.mult)

        def finish_da(j):
            e, b = divmod(j, PER_EXPERT)
            part_turned = turn_banks[j % BANKS]
            for t in range(PACK):
                nc.tensor.transpose(part_turned[:, t * P:(t + 1) * P], part[j][:, t * P:(t + 1) * P], ident[:])
            silu_neg = act_ring[j]
            nc.scalar.activation(
                silu_neg[:].rearrange("p (c u t) -> p c t u", u=2, t=PACK),
                a_block[j].rearrange("p t (c u) -> p c t u", u=2),
                ACT.Silu, scale=act_const[:],
            )
            nc.vector.scalar_tensor_tensor(
                out=da[e][:, b * H:(b + 1) * H].rearrange("p (s t) -> p s t", t=PACK),
                in0=silu_neg[:].rearrange("p (s t) -> p s t", t=PACK),
                scalar=1.0,
                in1=part_turned[:].rearrange("p (t s) -> p s t", t=PACK),
                op0=ALU.subtract, op1=ALU.mult,
            )

        def quantize_da(e, start, stop):
            nc.vector.quantize_mx(
                out=da_w[e][:, start:stop].bitcast(E5M2X4), scales=da_s[e][:, start:stop],
                in_=da[e][:, PACK * start:PACK * stop],
            )

        def second_product(kb, e):
            acc = mx_banks[e] if kb == 0 else turn_banks[e]
            nc.tensor.matmul_mx(
                out=acc[:],
                lhsT=w1_w[:, e, 2 * kb * P:2 * (kb + 1) * P].bitcast(E2M1X4),
                lhsT_scale=w1_s[:, e, kb * P:(kb + 1) * P],
                rhs=da_w[e][:].bitcast(E5M2X4), rhs_scale=da_s[e][:],
                start=True, stop=True,
            )
            nc.scalar.copy(dx[kb][:, e * C:(e + 1) * C], acc[:])

        for j in range(BLOCKS):
            e, b = divmod(j, PER_EXPERT)
            finish_da(j)
            if b == 0 and e > 0:
                quantize_da(e - 1, 0, C)
                second_product(0, e - 1)
            if b > 0 and e == LAST:
                quantize_da(LAST, (b - 1) * P, b * P)
        quantize_da(LAST, C - P, C)
        second_product(0, LAST)
        for kb in range(1, ROW_BLOCKS):
            for e in range(E):
                second_product(kb, e)

        cols = HALF // LIST_COL
        for kb in range(ROW_BLOCKS):
            for h in range(2):
                nc.vector.tensor_copy(first[h][:], dx[kb][:].indirect(pos1_sb[:, h * cols:(h + 1) * cols]))
            for h in range(2):
                both = total[2 * kb + h]
                nc.vector.tensor_tensor(
                    both[:], dx[kb][:].indirect(pos2_sb[:, h * cols:(h + 1) * cols]), first[h][:], ALU.add
                )
                nc.sync.dma_start(out=out[kb * P:(kb + 1) * P, h * HALF:(h + 1) * HALF], in_=both[:])
